import numpy as np
import ml_dtypes


def mxq(x, axis, fmt="e4m3"):
    dtype, down = {"e4m3": (ml_dtypes.float8_e4m3fn, 7), "e5m2": (ml_dtypes.float8_e5m2, 14)}[fmt]
    v = np.moveaxis(np.asarray(x, np.float32).astype(ml_dtypes.bfloat16).astype(np.float64), axis, -1)
    blocks = v.reshape(v.shape[:-1] + (-1, 32))
    amax = np.abs(blocks).max(-1, keepdims=True)
    byte = np.maximum(np.where(amax > 0, np.frexp(amax)[1] - 1 + 127, 0) - down, 1)
    scale = np.exp2(byte - 127.0)
    codes = (blocks / scale).astype(np.float32).astype(dtype).astype(np.float64)
    return np.moveaxis((codes * scale).reshape(v.shape), -1, axis)


WIDE = False


def mx_kscale(k):
    if not WIDE:
        return np.ones(k)
    levels = np.array([10, -10, 5, -5, 0])
    if k % 512:
        return np.exp2(np.random.permutation(np.resize(levels, k // 32))).repeat(32)
    a = np.empty((k // 512, 16))
    for p in range(k // 512):
        a[p, :8] = np.random.permutation(np.resize(levels, 8))
        for g in range(8):
            far = levels[np.abs(levels - a[p, g]) >= 10]
            a[p, g + 8] = far[np.random.randint(len(far))]
    return np.exp2(a.ravel()).repeat(32)


def f64(x):
    return np.asarray(x).astype(np.float64)


def striped(idx):
    return np.tile(idx.reshape(-1, 16).T, (8, 1)).astype(np.uint16)


def unstriped(offs):
    return offs[:16].T.reshape(-1).astype(np.int64)


def pack_weight(w):
    k, n = w.shape
    w = f64(np.asarray(w, np.float32).astype(ml_dtypes.bfloat16)).reshape(k // 32, 32, n)
    amax = np.abs(w).max(1)
    byte = np.clip(np.where(amax > 0, np.frexp(amax)[1] - 1 + 127 - 7, 1), 1, 254)
    scaled = (w * np.exp2(127.0 - byte)[:, None, :]).reshape(k, n).astype(np.float32)
    words = np.ascontiguousarray(scaled.reshape(k // 512, 128, 4, n).transpose(0, 1, 3, 2)).astype(ml_dtypes.float8_e4m3fn).view(np.uint8)
    return words, np.ascontiguousarray(byte.astype(np.uint8).reshape(k // 512, 16, n))


def unpack_weight(words, scales):
    g, p, n, _ = words.shape
    vals = np.ascontiguousarray(words).view(ml_dtypes.float8_e4m3fn).astype(np.float64) * np.repeat(np.exp2(scales.astype(np.float64) - 127.0), 8, axis=1)[..., None]
    return vals.transpose(0, 1, 3, 2).reshape(g * 512, n)


K, T, S, H, V, W = 512, 1024, 512, 512, 512, 2048
P = 2 ** 7


def setup_inputs():
    n = np.random.standard_normal
    s = mx_kscale(K)[:, None]
    u = mx_kscale(H)
    packed_xT = pack_weight(n((K, T)) * s)
    packed_eT = pack_weight(n((H, W)) / np.sqrt(H) / u[:, None])
    return {
        "x_words": packed_xT[0],
        "x_scales": packed_xT[1],
        "w1": (n((K, H)) / np.sqrt(K) / s * u).astype(np.float32),
        "e_words": packed_eT[0],
        "e_scales": packed_eT[1],
        "nn": (np.tile(np.random.uniform(1.5, 3.0, W), (P, 1))).astype(np.float32),
        "own": (np.random.uniform(1.5, 3.0, (S, 1))).astype(np.float32),
        "one": (np.tile(np.random.uniform(0.8, 1.2, V), (P, 1))).astype(np.float32),
        "pij": (np.random.uniform(0.0, 1.0, (S, V)) ** 2 * 3).astype(np.float32),
        "prec": (np.random.uniform(0.5, 1.5, (S, 1))).astype(np.float32),
        "offs": striped(np.random.permutation(T)[:S]),
        "lmk": striped(np.random.permutation(W)[:V]),
    }


def reference(x_words, x_scales, w1, e_words, e_scales, nn, own, one, pij, prec, offs, lmk):
    xq = unpack_weight(x_words, x_scales)[:, unstriped(offs)]
    h = mxq(f64(w1), 0, "e4m3").T @ xq
    e_lmk = unpack_weight(e_words, e_scales)[:, unstriped(lmk)]
    y = mxq(h, 0, "e4m3").T @ e_lmk
    dsq = f64(nn)[:1][:, unstriped(lmk)] - (0.6 * y) + f64(own)
    qn = f64(one)[:1] / (dsq + 1.0)
    qm = qn.mean(axis=1, keepdims=True)
    qr = qn / qm
    return (f64(pij) * (np.log(f64(pij) + 0.05) - np.log(qr))) * (f64(prec) * f64(one)[:1])

@@ -1,0 +1,221 @@
+from contextlib import ExitStack
+
+import concourse.mybir as mybir
+from concourse.masks import make_identity
+
+F32 = mybir.dt.float32
+BF16 = mybir.dt.bfloat16
+I32 = mybir.dt.int32
+U32 = mybir.dt.uint32
+U16 = mybir.dt.uint16
+U8 = mybir.dt.uint8
+FP8X4 = mybir.dt.float8_e4m3fn_x4
+ACT = mybir.ActivationFunctionType
+ALU = mybir.AluOpType
+
+P = 128
+PACK = 4
+K, T, S, H, V, W = 512, 1024, 512, 512, 512, 2048
+NB = 4
+HALF = 256
+
+FLOPS = 2 * K * H * S + 2 * H * S * V
+
+
+def tile_picked_ytsneg_div_p_kernel(
+    tc, x_words, x_scales, w1, e_words, e_scales, nn, own, one, pij, prec, offs, lmk, out
+):
+    nc = tc.nc
+    with ExitStack() as ctx:
+        sb = ctx.enter_context(tc.tile_pool(name="sb", bufs=1))
+        ps = ctx.enter_context(tc.psum_pool(name="ps", bufs=1))
+
+        def sbt(name, shape, dtype):
+            return sb.tile(shape, dtype, name=name, align_bytes=64)
+
+        def bank(tag, name, shape):
+            return ps.tile(shape, F32, name=name, tag=tag)
+
+        offs_sb = sb.tile([P, S // 16], U16, name="offs_sb")
+        lmk_sb = sb.tile([P, V // 16], U16, name="lmk_sb")
+        xs_win = sbt("xs_win", [P, T], U8)
+        es_win = sbt("es_win", [P, W], U8)
+        xw_win = sbt("xw_win", [P, T], I32)
+        ew_win = sbt("ew_win", [P, W], I32)
+        nn_win = sbt("nn_win", [P, W], F32)
+        rows = sbt("rows", [P, P], F32)
+        ident = sbt("ident", [P, P], F32)
+        warm = sbt("warm", [P, 2], F32)
+
+        nc.vector.memset(warm[:, 0:1], 1.0)
+        nc.scalar.activation(warm[:, 1:2], warm[:, 0:1], ACT.Abs_reciprocal_sqrt)
+        nc.gpsimd.memset(xs_win[:].bitcast(I32), 0)
+        nc.gpsimd.memset(rows[:], 0.0)
+        nc.vector.memset(es_win[:].bitcast(I32), 0)
+        nc.vector.memset(nn_win[:], 0.0)
+
+        w_raw = [sbt("w_raw%d" % h, [P, PACK, HALF], F32) for h in range(2)]
+
+        def load_w(h):
+            nc.sync.dma_start(w_raw[h][:], w1[:, h * HALF : (h + 1) * HALF].rearrange("(p j) c -> p j c", j=PACK))
+
+        nc.sync.dma_start(offs_sb[:], offs)
+        for q in range(4):
+            nc.sync.dma_start(xs_win[32 * q : 32 * q + 4, :].bitcast(I32), x_scales[0, 4 * q : 4 * q + 4, :].bitcast(I32))
+        nc.sync.dma_start(lmk_sb[:], lmk)
+        load_w(0)
+        load_w(1)
+        nc.gpsimd.dma_start(rows[0:4, :], own.rearrange("(b p) o -> b (p o)", b=NB))
+        nc.gpsimd.dma_start(rows[8:12, :], one[0:1, :].rearrange("o (b p) -> (o b) p", b=NB))
+        nc.gpsimd.dma_start(rows[4:8, :], prec.rearrange("(b p) o -> b (p o)", b=NB))
+        make_identity(nc, ident[:])
+        for q in range(4):
+            nc.gpsimd.dma_start(es_win[32 * q : 32 * q + 4, :].bitcast(I32), e_scales[0, 4 * q : 4 * q + 4, :].bitcast(I32))
+        nc.sync.dma_start(nn_win[0:1, :], nn[0:1, :])
+        nc.sync.dma_start(xw_win[:], x_words[0].rearrange("p n r -> p (n r)").bitcast(I32))
+        nc.sync.dma_start(ew_win[:], e_words[0].rearrange("p n r -> p (n r)").bitcast(I32))
+        one_sb = sbt("one_sb", [P, V], F32)
+        nc.sync.dma_start(one_sb[:], one)
+        pij_sb = []
+        for h in range(2):
+            pt = sbt("pij%d" % h, [P, 2, V], F32)
+            nc.sync.dma_start(pt[:], pij[h * HALF : (h + 1) * HALF, :].rearrange("(i p) v -> p i v", p=P))
+            pij_sb.extend([pt[:, 0, :], pt[:, 1, :]])
+
+        cols_ps = bank("y0", "cols_ps", [P, P])
+        nc.tensor.transpose(cols_ps[:], rows[:], ident[:])
+        cols = sbt("cols", [P, 12], F32)
+        nc.vector.tensor_copy(cols[:], cols_ps[:, 0:12])
+        inv_one = sbt("inv_one", [P, NB], F32)
+        nc.vector.reciprocal(inv_one[:], cols[:, 8:12])
+        y_scale = sbt("y_scale", [P, NB], F32)
+        nc.vector.tensor_scalar(y_scale[:], inv_one[:], -0.6, None, ALU.mult)
+        own_ps = bank("y3", "own_ps", [P, S])
+        for b in range(NB):
+            nc.tensor.transpose(own_ps[:, b * P : (b + 1) * P], cols[:, b : b + 1].to_broadcast([P, P]), ident[:])
+        xs = sbt("xs", [P, S], U8)
+        nc.vector.tensor_copy(xs[:], xs_win[:].indirect(offs_sb[:]))
+        nn_g = sbt("nn_g", [P, V], F32)
+        nc.vector.tensor_copy(nn_g[:], nn_win[:].indirect(lmk_sb[:]))
+
+        nn_ps = bank("y2", "nn_ps", [P, V])
+        for vb in range(NB):
+            nc.tensor.transpose(nn_ps[:, vb * P : (vb + 1) * P], nn_g[:, vb * P : (vb + 1) * P], ident[:])
+        y_bias = sbt("y_bias", [P, NB], F32)
+        nc.vector.scalar_tensor_tensor(y_bias[:], nn_ps[:, 0:V:P], 1.0, inv_one[:], ALU.add, ALU.mult)
+
+        w_bf = sbt("w_bf", [P, PACK, P, PACK], BF16)
+        for h in range(2):
+            nc.scalar.copy(
+                w_bf[:, :, h * 64 : (h + 1) * 64, :].rearrange("p t m j -> p m t j"),
+                w_raw[h][:].rearrange("p j (m t) -> p m t j", t=PACK),
+            )
+        xq = []
+        for h in range(2):
+            xh = sbt("xq%d" % h, [P, HALF], U32)
+            nc.vector.tensor_copy(xh[:], xw_win[:].bitcast(U32).indirect(offs_sb[:, 16 * h : 16 * (h + 1)]))
+            xq.append(xh)
+
+        wq = sbt("wq", [P, H], U32)
+        ws = sbt("ws", [P, H], U8)
+        nc.vector.quantize_mx(out=wq[:].bitcast(FP8X4), scales=ws[:], in_=w_bf[:].rearrange("p t m j -> p (t m j)"))
+
+        u_ps = [bank("u%d" % b, "u_ps%d" % b, [P, V]) for b in range(NB)]
+        for vb in range(NB):
+            ot = sbt("own_term%d" % vb, [P, S], F32)
+            nc.scalar.activation(ot[:], own_ps[:], ACT.Copy, scale=inv_one[:, vb : vb + 1])
+            for tb in range(NB):
+                nc.tensor.matmul(
+                    u_ps[tb][:, vb * P : (vb + 1) * P], lhsT=ot[:, tb * P : (tb + 1) * P], rhs=ident[:],
+                    start=(vb == 0), stop=False, is_transpose=True,
+                )
+
+        es = sbt("es", [P, V], U8)
+        nc.vector.tensor_copy(es[:], es_win[:].indirect(lmk_sb[:]))
+
+        hq = []
+        hs = []
+        for h in range(2):
+            h_bf = sbt("h_bf%d" % h, [P, HALF, PACK], BF16)
+            for i in range(2):
+                tb = 2 * h + i
+                h_ps = bank("y%d" % tb, "h_ps%d" % tb, [P, PACK, P])
+                for t in range(PACK):
+                    nc.tensor.matmul_mx(
+                        out=h_ps[:, t, :],
+                        lhsT=wq[:, t * P : (t + 1) * P].bitcast(FP8X4), lhsT_scale=ws[:, t * P : (t + 1) * P],
+                        rhs=xq[h][:, i * P : (i + 1) * P].bitcast(FP8X4), rhs_scale=xs[:, tb * P : (tb + 1) * P],
+                        start=True, stop=True,
+                    )
+                nc.scalar.copy(h_bf[:, i * P : (i + 1) * P, :], h_ps[:].rearrange("p j n -> p n j"))
+            hqh = sbt("hq%d" % h, [P, HALF], U32)
+            hsh = sbt("hs%d" % h, [P, HALF], U8)
+            nc.vector.quantize_mx(out=hqh[:].bitcast(FP8X4), scales=hsh[:], in_=h_bf[:].rearrange("p n j -> p (n j)"))
+            hq.append(hqh)
+            hs.append(hsh)
+
+        eq = []
+        for g in range(2):
+            eh = sbt("eq%d" % g, [P, HALF], U32)
+            nc.vector.tensor_copy(eh[:], ew_win[:].bitcast(U32).indirect(lmk_sb[:, 16 * g : 16 * (g + 1)]))
+            eq.append(eh)
+
+        rs = []
+        for h in range(2):
+            a_sb = []
+            for g in range(2):
+                y_ps = bank("y%d" % (2 * h + g), "y_ps%d%d" % (h, g), [P, 2, HALF])
+                for i in range(2):
+                    vb = 2 * g + i
+                    nc.tensor.matmul_mx(
+                        out=y_ps[:, i, :],
+                        lhsT=eq[g][:, i * P : (i + 1) * P].bitcast(FP8X4), lhsT_scale=es[:, vb * P : (vb + 1) * P],
+                        rhs=hq[h][:].bitcast(FP8X4), rhs_scale=hs[h][:],
+                        start=True, stop=True,
+                    )
+                for i in range(2):
+                    vb = 2 * g + i
+                    at = sbt("a%d%d" % (h, vb), [P, HALF], F32)
+                    if h == 0 and g == 0:
+                        nc.scalar.activation(
+                            at[:], y_ps[:, i, :], ACT.Identity, bias=y_bias[:, vb : vb + 1], scale=y_scale[:, vb : vb + 1]
+                        )
+                    else:
+                        nc.vector.tensor_scalar(
+                            at[:], y_ps[:, i, :], y_scale[:, vb : vb + 1], y_bias[:, vb : vb + 1], ALU.mult, ALU.add
+                        )
+                    a_sb.append(at)
+            for i in range(2):
+                tb = 2 * h + i
+                for vb in range(NB):
+                    nc.tensor.matmul(
+                        u_ps[tb][:, vb * P : (vb + 1) * P], lhsT=a_sb[vb][:, i * P : (i + 1) * P], rhs=ident[:],
+                        start=False, stop=(vb == NB - 1), is_transpose=True,
+                    )
+                rt = sbt("rs%d" % tb, [P, V], F32)
+                nc.scalar.activation(rt[:], u_ps[tb][:], ACT.Abs_reciprocal_sqrt)
+                rs.append(rt)
+
+        qsum = sbt("qsum", [P, NB], F32)
+        qn = sbt("qn", [P, V], F32)
+        arg = []
+        weight = []
+        for tb in range(NB):
+            nc.vector.scalar_tensor_tensor(
+                qn[:], rs[tb][:], 1.0, rs[tb][:], ALU.mult, ALU.mult, accum_out=qsum[:, tb : tb + 1]
+            )
+        qm = sbt("qm", [P, NB], F32)
+        nc.vector.tensor_scalar(qm[:], qsum[:], 1.0 / V, None, ALU.mult)
+        for tb in range(NB):
+            wt = sbt("weight%d" % tb, [P, V], F32)
+            nc.gpsimd.tensor_tensor(wt[:], pij_sb[tb], one_sb[:], ALU.mult)
+            weight.append(wt)
+            at = sbt("arg%d" % tb, [P, V], F32)
+            nc.vector.scalar_tensor_tensor(at[:], pij_sb[tb], 0.05, u_ps[tb][:], ALU.add, ALU.mult)
+            arg.append(at)
+        for tb in range(NB):
+            lg = sbt("lg%d" % tb, [P, V], F32)
+            nc.scalar.activation(lg[:], arg[tb][:], ACT.Ln, scale=qm[:, tb : tb + 1])
+            res = sbt("res%d" % tb, [P, V], F32)
+            nc.vector.scalar_tensor_tensor(res[:], lg[:], cols[:, 4 + tb : 5 + tb], weight[tb][:], ALU.mult, ALU.mult)
+            nc.sync.dma_start(out[tb * P : (tb + 1) * P, :], res[:])

@@ -30,8 +30,8 @@ def tile_picked_ytsneg_div_p_kernel(
         sb = ctx.enter_context(tc.tile_pool(name="sb", bufs=1))
         ps = ctx.enter_context(tc.psum_pool(name="ps", bufs=1))
 
-        def sbt(name, shape, dtype):
-            return sb.tile(shape, dtype, name=name, align_bytes=64)
+        def sbt(name, shape, dtype, tag=None):
+            return sb.tile(shape, dtype, name=name, tag=tag or name, align_bytes=64)
 
         def bank(tag, name, shape):
             return ps.tile(shape, F32, name=name, tag=tag)
@@ -41,61 +41,70 @@ def tile_picked_ytsneg_div_p_kernel(
         xs_win = sbt("xs_win", [P, T], U8)
         es_win = sbt("es_win", [P, W], U8)
         xw_win = sbt("xw_win", [P, T], I32)
-        ew_win = sbt("ew_win", [P, W], I32)
         nn_win = sbt("nn_win", [P, W], F32)
-        rows = sbt("rows", [P, P], F32)
+        own_sb = sbt("own_sb", [P, NB], F32)
+        one_sb = sbt("one_sb", [P, V], F32)
         ident = sbt("ident", [P, P], F32)
-        warm = sbt("warm", [P, 2], F32)
+        v_squared = sbt("v_squared", [P, 1], F32)
+        inv_v = sbt("inv_v", [P, 1], F32)
 
-        nc.vector.memset(warm[:, 0:1], 1.0)
-        nc.scalar.activation(warm[:, 1:2], warm[:, 0:1], ACT.Abs_reciprocal_sqrt)
+        nc.gpsimd.memset(v_squared[:], float(V * V))
         nc.gpsimd.memset(xs_win[:].bitcast(I32), 0)
-        nc.gpsimd.memset(rows[:], 0.0)
-        nc.vector.memset(es_win[:].bitcast(I32), 0)
         nc.vector.memset(nn_win[:], 0.0)
+        make_identity(nc, ident[:])
+        nc.gpsimd.memset(es_win[:].bitcast(I32), 0)
 
         w_raw = [sbt("w_raw%d" % h, [P, PACK, HALF], F32) for h in range(2)]
 
         def load_w(h):
             nc.sync.dma_start(w_raw[h][:], w1[:, h * HALF : (h + 1) * HALF].rearrange("(p j) c -> p j c", j=PACK))
 
+        inv_v0 = sbt("inv_v0", [P, 2], F32)
+        nc.scalar.activation(inv_v0[:, 0:1], v_squared[:], ACT.Abs_reciprocal_sqrt)
+        nc.vector.tensor_scalar(inv_v0[:, 1:2], inv_v0[:, 0:1], -float(V), 2.0, ALU.mult, ALU.add)
+        nc.vector.tensor_tensor(inv_v[:], inv_v0[:, 0:1], inv_v0[:, 1:2], ALU.mult)
         nc.sync.dma_start(offs_sb[:], offs)
-        for q in range(4):
-            nc.sync.dma_start(xs_win[32 * q : 32 * q + 4, :].bitcast(I32), x_scales[0, 4 * q : 4 * q + 4, :].bitcast(I32))
         nc.sync.dma_start(lmk_sb[:], lmk)
+        nc.sync.dma_start(own_sb[:], own.rearrange("(p b) o -> p (b o)", b=NB))
+        nc.sync.dma_start(one_sb[:], one)
+        nc.sync.dma_start(xw_win[:], x_words[0].rearrange("p n r -> p (n r)").bitcast(I32))
         load_w(0)
         load_w(1)
-        nc.gpsimd.dma_start(rows[0:4, :], own.rearrange("(b p) o -> b (p o)", b=NB))
-        nc.gpsimd.dma_start(rows[8:12, :], one[0:1, :].rearrange("o (b p) -> (o b) p", b=NB))
-        nc.gpsimd.dma_start(rows[4:8, :], prec.rearrange("(b p) o -> b (p o)", b=NB))
-        make_identity(nc, ident[:])
+        for q in range(4):
+            nc.scalar.dma_start(xs_win[32 * q : 32 * q + 4, :].bitcast(I32), x_scales[0, 4 * q : 4 * q + 4, :].bitcast(I32))
+        nc.scalar.dma_start(nn_win[0:1, :], nn[0:1, :])
         for q in range(4):
             nc.gpsimd.dma_start(es_win[32 * q : 32 * q + 4, :].bitcast(I32), e_scales[0, 4 * q : 4 * q + 4, :].bitcast(I32))
-        nc.sync.dma_start(nn_win[0:1, :], nn[0:1, :])
-        nc.sync.dma_start(xw_win[:], x_words[0].rearrange("p n r -> p (n r)").bitcast(I32))
-        nc.sync.dma_start(ew_win[:], e_words[0].rearrange("p n r -> p (n r)").bitcast(I32))
-        one_sb = sbt("one_sb", [P, V], F32)
-        nc.sync.dma_start(one_sb[:], one)
-        pij_sb = []
-        for h in range(2):
-            pt = sbt("pij%d" % h, [P, 2, V], F32)
-            nc.sync.dma_start(pt[:], pij[h * HALF : (h + 1) * HALF, :].rearrange("(i p) v -> p i v", p=P))
-            pij_sb.extend([pt[:, 0, :], pt[:, 1, :]])
 
-        cols_ps = bank("y0", "cols_ps", [P, P])
-        nc.tensor.transpose(cols_ps[:], rows[:], ident[:])
-        cols = sbt("cols", [P, 12], F32)
-        nc.vector.tensor_copy(cols[:], cols_ps[:, 0:12])
-        inv_one = sbt("inv_one", [P, NB], F32)
-        nc.vector.reciprocal(inv_one[:], cols[:, 8:12])
-        y_scale = sbt("y_scale", [P, NB], F32)
-        nc.vector.tensor_scalar(y_scale[:], inv_one[:], -0.6, None, ALU.mult)
-        own_ps = bank("y3", "own_ps", [P, S])
+        own_ps = bank("u3", "own_ps", [P, S])
         for b in range(NB):
-            nc.tensor.transpose(own_ps[:, b * P : (b + 1) * P], cols[:, b : b + 1].to_broadcast([P, P]), ident[:])
-        xs = sbt("xs", [P, S], U8)
+            nc.tensor.transpose(own_ps[:, b:S:NB], own_sb[:, b : b + 1].to_broadcast([P, P]), ident[:])
+        ew_win = sbt("ew_win", [P, W], I32, tag="own_sb")
+        nc.sync.dma_start(ew_win[:], e_words[0].rearrange("p n r -> p (n r)").bitcast(I32))
+        one_ps = bank("y1", "one_ps", [P, V])
+        for vb in range(NB):
+            nc.tensor.transpose(one_ps[:, vb * P : (vb + 1) * P], one_sb[:, vb * P : (vb + 1) * P], ident[:])
+        inv_raw = sbt("inv_raw", [P, NB], F32)
+        nc.vector.reciprocal(inv_raw[:], one_ps[:, 0:V:P])
+        inv_first = sbt("inv_first", [P, 2], F32)
+        nc.vector.tensor_copy(inv_first[:], inv_raw[:, 0:2])
+        inv_one = sbt("inv_one", [P, NB], F32)
+        nc.vector.tensor_copy(inv_one[:], inv_raw[:])
+        y_scale = sbt("y_scale", [P, NB], F32)
+        nc.vector.tensor_scalar(y_scale[:], inv_raw[:], -0.6, None, ALU.mult)
+
+        own_term = [sbt("own_term%d" % vb, [P, S], F32) for vb in range(NB)]
+        for vb in range(2):
+            nc.scalar.activation(own_term[vb][:], own_ps[:], ACT.Copy, scale=inv_first[:, vb : vb + 1])
+
+        xq = sbt("xq", [P, S], U32, tag="inv_raw")
+        for h in range(2):
+            nc.vector.tensor_copy(
+                xq[:, h * HALF : (h + 1) * HALF], xw_win[:].bitcast(U32).indirect(offs_sb[:, 16 * h : 16 * (h + 1)])
+            )
+        xs = sbt("xs", [P, S], U8, tag="xw_win")
         nc.vector.tensor_copy(xs[:], xs_win[:].indirect(offs_sb[:]))
-        nn_g = sbt("nn_g", [P, V], F32)
+        nn_g = sbt("nn_g", [P, V], F32, tag="xs_win")
         nc.vector.tensor_copy(nn_g[:], nn_win[:].indirect(lmk_sb[:]))
 
         nn_ps = bank("y2", "nn_ps", [P, V])
@@ -104,35 +113,27 @@ def tile_picked_ytsneg_div_p_kernel(
         y_bias = sbt("y_bias", [P, NB], F32)
         nc.vector.scalar_tensor_tensor(y_bias[:], nn_ps[:, 0:V:P], 1.0, inv_one[:], ALU.add, ALU.mult)
 
-        w_bf = sbt("w_bf", [P, PACK, P, PACK], BF16)
+        w_bf = sbt("w_bf", [P, PACK, P, PACK], BF16, tag="inv_first")
         for h in range(2):
             nc.scalar.copy(
                 w_bf[:, :, h * 64 : (h + 1) * 64, :].rearrange("p t m j -> p m t j"),
                 w_raw[h][:].rearrange("p j (m t) -> p m t j", t=PACK),
             )
-        xq = []
+        for vb in range(2, NB):
+            nc.scalar.activation(own_term[vb][:], own_ps[:], ACT.Copy, scale=inv_one[:, vb : vb + 1])
+        pij_sb = []
         for h in range(2):
-            xh = sbt("xq%d" % h, [P, HALF], U32)
-            nc.vector.tensor_copy(xh[:], xw_win[:].bitcast(U32).indirect(offs_sb[:, 16 * h : 16 * (h + 1)]))
-            xq.append(xh)
-
+            pt = sbt("pij%d" % h, [P, 2, V], F32, tag="w_raw%d" % h)
+            nc.sync.dma_start(pt[:], pij[h * HALF : (h + 1) * HALF, :].rearrange("(i p) v -> p i v", p=P))
+            pij_sb.extend([pt[:, 0, :], pt[:, 1, :]])
         wq = sbt("wq", [P, H], U32)
         ws = sbt("ws", [P, H], U8)
         nc.vector.quantize_mx(out=wq[:].bitcast(FP8X4), scales=ws[:], in_=w_bf[:].rearrange("p t m j -> p (t m j)"))
 
-        u_ps = [bank("u%d" % b, "u_ps%d" % b, [P, V]) for b in range(NB)]
-        for vb in range(NB):
-            ot = sbt("own_term%d" % vb, [P, S], F32)
-            nc.scalar.activation(ot[:], own_ps[:], ACT.Copy, scale=inv_one[:, vb : vb + 1])
-            for tb in range(NB):
-                nc.tensor.matmul(
-                    u_ps[tb][:, vb * P : (vb + 1) * P], lhsT=ot[:, tb * P : (tb + 1) * P], rhs=ident[:],
-                    start=(vb == 0), stop=False, is_transpose=True,
-                )
 
-        es = sbt("es", [P, V], U8)
-        nc.vector.tensor_copy(es[:], es_win[:].indirect(lmk_sb[:]))
-
+        prec_sb = sbt("prec_sb", [P, NB], F32, tag="nn_win")
+        with nc.allow_non_contiguous_dma(reason="one value to a partition"):
+            nc.sync.dma_start(prec_sb[:], prec.rearrange("(b p) o -> p (b o)", b=NB))
         hq = []
         hs = []
         for h in range(2):
@@ -144,7 +145,7 @@ def tile_picked_ytsneg_div_p_kernel(
                     nc.tensor.matmul_mx(
                         out=h_ps[:, t, :],
                         lhsT=wq[:, t * P : (t + 1) * P].bitcast(FP8X4), lhsT_scale=ws[:, t * P : (t + 1) * P],
-                        rhs=xq[h][:, i * P : (i + 1) * P].bitcast(FP8X4), rhs_scale=xs[:, tb * P : (tb + 1) * P],
+                        rhs=xq[:, tb * P : (tb + 1) * P].bitcast(FP8X4), rhs_scale=xs[:, tb * P : (tb + 1) * P],
                         start=True, stop=True,
                     )
                 nc.scalar.copy(h_bf[:, i * P : (i + 1) * P, :], h_ps[:].rearrange("p j n -> p n j"))
@@ -154,29 +155,43 @@ def tile_picked_ytsneg_div_p_kernel(
             hq.append(hqh)
             hs.append(hsh)
 
-        eq = []
+        u_ps = [bank("u%d" % b, "u_ps%d" % b, [P, V]) for b in range(NB)]
+        for tb in range(NB):
+            for vb in range(NB):
+                nc.tensor.matmul(
+                    u_ps[tb][:, vb * P : (vb + 1) * P], lhsT=own_term[vb][:, tb * P : (tb + 1) * P], rhs=ident[:],
+                    start=(vb == 0), stop=False, is_transpose=True,
+                )
+        es = sbt("es", [P, V], U8, tag="inv_first")
+        nc.vector.tensor_copy(es[:], es_win[:].indirect(lmk_sb[:]))
+        eq = sbt("eq", [P, V], U32, tag="es_win")
         for g in range(2):
-            eh = sbt("eq%d" % g, [P, HALF], U32)
-            nc.vector.tensor_copy(eh[:], ew_win[:].bitcast(U32).indirect(lmk_sb[:, 16 * g : 16 * (g + 1)]))
-            eq.append(eh)
+            nc.vector.tensor_copy(
+                eq[:, g * HALF : (g + 1) * HALF], ew_win[:].bitcast(U32).indirect(lmk_sb[:, 16 * g : 16 * (g + 1)])
+            )
 
         rs = []
+        qsum = sbt("qsum", [P, NB], F32)
+        lg = [sbt("lg%d" % tb, [P, V], F32) for tb in range(NB)]
+        nc.gpsimd.memset(lg[0][:, 0:1], 0.0)
+        a_all = []
         for h in range(2):
             a_sb = []
+            a_all.append(a_sb)
             for g in range(2):
                 y_ps = bank("y%d" % (2 * h + g), "y_ps%d%d" % (h, g), [P, 2, HALF])
                 for i in range(2):
                     vb = 2 * g + i
                     nc.tensor.matmul_mx(
                         out=y_ps[:, i, :],
-                        lhsT=eq[g][:, i * P : (i + 1) * P].bitcast(FP8X4), lhsT_scale=es[:, vb * P : (vb + 1) * P],
+                        lhsT=eq[:, vb * P : (vb + 1) * P].bitcast(FP8X4), lhsT_scale=es[:, vb * P : (vb + 1) * P],
                         rhs=hq[h][:].bitcast(FP8X4), rhs_scale=hs[h][:],
                         start=True, stop=True,
                     )
                 for i in range(2):
                     vb = 2 * g + i
                     at = sbt("a%d%d" % (h, vb), [P, HALF], F32)
-                    if h == 0 and g == 0:
+                    if g == 0:
                         nc.scalar.activation(
                             at[:], y_ps[:, i, :], ACT.Identity, bias=y_bias[:, vb : vb + 1], scale=y_scale[:, vb : vb + 1]
                         )
@@ -185,6 +200,8 @@ def tile_picked_ytsneg_div_p_kernel(
                             at[:], y_ps[:, i, :], y_scale[:, vb : vb + 1], y_bias[:, vb : vb + 1], ALU.mult, ALU.add
                         )
                     a_sb.append(at)
+        for h in range(2):
+            a_sb = a_all[h]
             for i in range(2):
                 tb = 2 * h + i
                 for vb in range(NB):
@@ -193,29 +210,35 @@ def tile_picked_ytsneg_div_p_kernel(
                         start=False, stop=(vb == NB - 1), is_transpose=True,
                     )
                 rt = sbt("rs%d" % tb, [P, V], F32)
-                nc.scalar.activation(rt[:], u_ps[tb][:], ACT.Abs_reciprocal_sqrt)
+                nc.scalar.activation(rt[:], u_ps[tb][:], ACT.Abs_reciprocal_sqrt, bias=lg[0][:, 0:1])
                 rs.append(rt)
+                if tb == 1:
+                    qn_first = sbt("qn_first", [P, V], F32)
+                    nc.scalar.activation(qn_first[:], rs[0][:], ACT.Square, scale=V**-0.5, accum_out=qsum[:, 0:1])
 
-        qsum = sbt("qsum", [P, NB], F32)
-        qn = sbt("qn", [P, V], F32)
-        arg = []
-        weight = []
-        for tb in range(NB):
+        qn = sbt("qn", [P, V], F32, tag="y_bias")
+        late = sbt("late", [P, 2, NB, V], F32, tag="y_scale")
+        arg = late[:, 0]
+        weight = late[:, 1]
+        nc.vector.scalar_tensor_tensor(arg[:, 0, :], pij_sb[0], 0.05, u_ps[0][:], ALU.add, ALU.mult)
+        for tb in range(1, NB):
             nc.vector.scalar_tensor_tensor(
-                qn[:], rs[tb][:], 1.0, rs[tb][:], ALU.mult, ALU.mult, accum_out=qsum[:, tb : tb + 1]
+                qn[:], rs[tb][:], inv_v[:], rs[tb][:], ALU.mult, ALU.mult, accum_out=qsum[:, tb : tb + 1]
             )
         qm = sbt("qm", [P, NB], F32)
-        nc.vector.tensor_scalar(qm[:], qsum[:], 1.0 / V, None, ALU.mult)
+        nc.vector.tensor_copy(qm[:], qsum[:])
         for tb in range(NB):
-            wt = sbt("weight%d" % tb, [P, V], F32)
-            nc.gpsimd.tensor_tensor(wt[:], pij_sb[tb], one_sb[:], ALU.mult)
-            weight.append(wt)
-            at = sbt("arg%d" % tb, [P, V], F32)
-            nc.vector.scalar_tensor_tensor(at[:], pij_sb[tb], 0.05, u_ps[tb][:], ALU.add, ALU.mult)
-            arg.append(at)
-        for tb in range(NB):
-            lg = sbt("lg%d" % tb, [P, V], F32)
-            nc.scalar.activation(lg[:], arg[tb][:], ACT.Ln, scale=qm[:, tb : tb + 1])
-            res = sbt("res%d" % tb, [P, V], F32)
-            nc.vector.scalar_tensor_tensor(res[:], lg[:], cols[:, 4 + tb : 5 + tb], weight[tb][:], ALU.mult, ALU.mult)
-            nc.sync.dma_start(out[tb * P : (tb + 1) * P, :], res[:])
+            nc.vector.tensor_tensor(weight[:, tb, :], pij_sb[tb], one_sb[:], ALU.mult)
+            if tb + 1 < NB:
+                nc.vector.scalar_tensor_tensor(
+                    arg[:, tb + 1, :], pij_sb[tb + 1], 0.05, u_ps[tb + 1][:], ALU.add, ALU.mult
+                )
+        pieces = [(tb, 0, V) for tb in range(NB - 1)] + [(NB - 1, 0, HALF), (NB - 1, HALF, V)]
+        for tb, c0, c1 in pieces:
+            mean = qsum if tb == 0 else qm
+            nc.scalar.activation(lg[tb][:, c0:c1], arg[:, tb, c0:c1], ACT.Ln, scale=mean[:, tb : tb + 1])
+            res = sbt("res%d_%d" % (tb, c0), [P, c1 - c0], F32)
+            nc.vector.scalar_tensor_tensor(
+                res[:], lg[tb][:, c0:c1], prec_sb[:, tb : tb + 1], weight[:, tb, c0:c1], ALU.mult, ALU.mult
+            )
+            nc.sync.dma_start(out[tb * P : (tb + 1) * P, c0:c1], res[:])

from contextlib import ExitStack

import concourse.mybir as mybir
from concourse.masks import make_identity

F32 = mybir.dt.float32
BF16 = mybir.dt.bfloat16
I32 = mybir.dt.int32
U32 = mybir.dt.uint32
U16 = mybir.dt.uint16
U8 = mybir.dt.uint8
FP8X4 = mybir.dt.float8_e4m3fn_x4
ACT = mybir.ActivationFunctionType
ALU = mybir.AluOpType

P = 128
PACK = 4
K, T, S, H, V, W = 512, 1024, 512, 512, 512, 2048
NB = 4
HALF = 256

FLOPS = 2 * K * H * S + 2 * H * S * V


def tile_picked_ytsneg_div_p_kernel(
    tc, x_words, x_scales, w1, e_words, e_scales, nn, own, one, pij, prec, offs, lmk, out
):
    nc = tc.nc
    with ExitStack() as ctx:
        sb = ctx.enter_context(tc.tile_pool(name="sb", bufs=1))
        ps = ctx.enter_context(tc.psum_pool(name="ps", bufs=1))

        def sbt(name, shape, dtype, tag=None):
            return sb.tile(shape, dtype, name=name, tag=tag or name, align_bytes=64)

        def bank(tag, name, shape):
            return ps.tile(shape, F32, name=name, tag=tag)

        offs_sb = sb.tile([P, S // 16], U16, name="offs_sb")
        lmk_sb = sb.tile([P, V // 16], U16, name="lmk_sb")
        xs_win = sbt("xs_win", [P, T], U8)
        es_win = sbt("es_win", [P, W], U8)
        xw_win = sbt("xw_win", [P, T], I32)
        nn_win = sbt("nn_win", [P, W], F32)
        own_sb = sbt("own_sb", [P, NB], F32)
        one_sb = sbt("one_sb", [P, V], F32)
        ident = sbt("ident", [P, P], F32)
        v_squared = sbt("v_squared", [P, 1], F32)
        inv_v = sbt("inv_v", [P, 1], F32)

        nc.gpsimd.memset(v_squared[:], float(V * V))
        nc.gpsimd.memset(xs_win[:].bitcast(I32), 0)
        nc.vector.memset(nn_win[:], 0.0)
        make_identity(nc, ident[:])
        nc.gpsimd.memset(es_win[:].bitcast(I32), 0)

        w_raw = [sbt("w_raw%d" % h, [P, PACK, HALF], F32) for h in range(2)]

        def load_w(h):
            nc.sync.dma_start(w_raw[h][:], w1[:, h * HALF : (h + 1) * HALF].rearrange("(p j) c -> p j c", j=PACK))

        inv_v0 = sbt("inv_v0", [P, 2], F32)
        nc.scalar.activation(inv_v0[:, 0:1], v_squared[:], ACT.Abs_reciprocal_sqrt)
        nc.vector.tensor_scalar(inv_v0[:, 1:2], inv_v0[:, 0:1], -float(V), 2.0, ALU.mult, ALU.add)
        nc.vector.tensor_tensor(inv_v[:], inv_v0[:, 0:1], inv_v0[:, 1:2], ALU.mult)
        nc.sync.dma_start(offs_sb[:], offs)
        nc.sync.dma_start(lmk_sb[:], lmk)
        nc.sync.dma_start(own_sb[:], own.rearrange("(p b) o -> p (b o)", b=NB))
        nc.sync.dma_start(one_sb[:], one)
        nc.sync.dma_start(xw_win[:], x_words[0].rearrange("p n r -> p (n r)").bitcast(I32))
        load_w(0)
        load_w(1)
        for q in range(4):
            nc.scalar.dma_start(xs_win[32 * q : 32 * q + 4, :].bitcast(I32), x_scales[0, 4 * q : 4 * q + 4, :].bitcast(I32))
        nc.scalar.dma_start(nn_win[0:1, :], nn[0:1, :])
        for q in range(4):
            nc.gpsimd.dma_start(es_win[32 * q : 32 * q + 4, :].bitcast(I32), e_scales[0, 4 * q : 4 * q + 4, :].bitcast(I32))

        own_ps = bank("u3", "own_ps", [P, S])
        for b in range(NB):
            nc.tensor.transpose(own_ps[:, b:S:NB], own_sb[:, b : b + 1].to_broadcast([P, P]), ident[:])
        ew_win = sbt("ew_win", [P, W], I32, tag="own_sb")
        nc.sync.dma_start(ew_win[:], e_words[0].rearrange("p n r -> p (n r)").bitcast(I32))
        one_ps = bank("y1", "one_ps", [P, V])
        for vb in range(NB):
            nc.tensor.transpose(one_ps[:, vb * P : (vb + 1) * P], one_sb[:, vb * P : (vb + 1) * P], ident[:])
        inv_raw = sbt("inv_raw", [P, NB], F32)
        nc.vector.reciprocal(inv_raw[:], one_ps[:, 0:V:P])
        inv_first = sbt("inv_first", [P, 2], F32)
        nc.vector.tensor_copy(inv_first[:], inv_raw[:, 0:2])
        inv_one = sbt("inv_one", [P, NB], F32)
        nc.vector.tensor_copy(inv_one[:], inv_raw[:])
        y_scale = sbt("y_scale", [P, NB], F32)
        nc.vector.tensor_scalar(y_scale[:], inv_raw[:], -0.6, None, ALU.mult)

        own_term = [sbt("own_term%d" % vb, [P, S], F32) for vb in range(NB)]
        for vb in range(2):
            nc.scalar.activation(own_term[vb][:], own_ps[:], ACT.Copy, scale=inv_first[:, vb : vb + 1])

        xq = sbt("xq", [P, S], U32, tag="inv_raw")
        for h in range(2):
            nc.vector.tensor_copy(
                xq[:, h * HALF : (h + 1) * HALF], xw_win[:].bitcast(U32).indirect(offs_sb[:, 16 * h : 16 * (h + 1)])
            )
        xs = sbt("xs", [P, S], U8, tag="xw_win")
        nc.vector.tensor_copy(xs[:], xs_win[:].indirect(offs_sb[:]))
        nn_g = sbt("nn_g", [P, V], F32, tag="xs_win")
        nc.vector.tensor_copy(nn_g[:], nn_win[:].indirect(lmk_sb[:]))

        nn_ps = bank("y2", "nn_ps", [P, V])
        for vb in range(NB):
            nc.tensor.transpose(nn_ps[:, vb * P : (vb + 1) * P], nn_g[:, vb * P : (vb + 1) * P], ident[:])
        y_bias = sbt("y_bias", [P, NB], F32)
        nc.vector.scalar_tensor_tensor(y_bias[:], nn_ps[:, 0:V:P], 1.0, inv_one[:], ALU.add, ALU.mult)

        w_bf = sbt("w_bf", [P, PACK, P, PACK], BF16, tag="inv_first")
        for h in range(2):
            nc.scalar.copy(
                w_bf[:, :, h * 64 : (h + 1) * 64, :].rearrange("p t m j -> p m t j"),
                w_raw[h][:].rearrange("p j (m t) -> p m t j", t=PACK),
            )
        for vb in range(2, NB):
            nc.scalar.activation(own_term[vb][:], own_ps[:], ACT.Copy, scale=inv_one[:, vb : vb + 1])
        pij_sb = []
        for h in range(2):
            pt = sbt("pij%d" % h, [P, 2, V], F32, tag="w_raw%d" % h)
            nc.sync.dma_start(pt[:], pij[h * HALF : (h + 1) * HALF, :].rearrange("(i p) v -> p i v", p=P))
            pij_sb.extend([pt[:, 0, :], pt[:, 1, :]])
        wq = sbt("wq", [P, H], U32)
        ws = sbt("ws", [P, H], U8)
        nc.vector.quantize_mx(out=wq[:].bitcast(FP8X4), scales=ws[:], in_=w_bf[:].rearrange("p t m j -> p (t m j)"))


        prec_sb = sbt("prec_sb", [P, NB], F32, tag="nn_win")
        with nc.allow_non_contiguous_dma(reason="one value to a partition"):
            nc.sync.dma_start(prec_sb[:], prec.rearrange("(b p) o -> p (b o)", b=NB))
        hq = []
        hs = []
        for h in range(2):
            h_bf = sbt("h_bf%d" % h, [P, HALF, PACK], BF16)
            for i in range(2):
                tb = 2 * h + i
                h_ps = bank("y%d" % tb, "h_ps%d" % tb, [P, PACK, P])
                for t in range(PACK):
                    nc.tensor.matmul_mx(
                        out=h_ps[:, t, :],
                        lhsT=wq[:, t * P : (t + 1) * P].bitcast(FP8X4), lhsT_scale=ws[:, t * P : (t + 1) * P],
                        rhs=xq[:, tb * P : (tb + 1) * P].bitcast(FP8X4), rhs_scale=xs[:, tb * P : (tb + 1) * P],
                        start=True, stop=True,
                    )
                nc.scalar.copy(h_bf[:, i * P : (i + 1) * P, :], h_ps[:].rearrange("p j n -> p n j"))
            hqh = sbt("hq%d" % h, [P, HALF], U32)
            hsh = sbt("hs%d" % h, [P, HALF], U8)
            nc.vector.quantize_mx(out=hqh[:].bitcast(FP8X4), scales=hsh[:], in_=h_bf[:].rearrange("p n j -> p (n j)"))
            hq.append(hqh)
            hs.append(hsh)

        u_ps = [bank("u%d" % b, "u_ps%d" % b, [P, V]) for b in range(NB)]
        for tb in range(NB):
            for vb in range(NB):
                nc.tensor.matmul(
                    u_ps[tb][:, vb * P : (vb + 1) * P], lhsT=own_term[vb][:, tb * P : (tb + 1) * P], rhs=ident[:],
                    start=(vb == 0), stop=False, is_transpose=True,
                )
        es = sbt("es", [P, V], U8, tag="inv_first")
        nc.vector.tensor_copy(es[:], es_win[:].indirect(lmk_sb[:]))
        eq = sbt("eq", [P, V], U32, tag="es_win")
        for g in range(2):
            nc.vector.tensor_copy(
                eq[:, g * HALF : (g + 1) * HALF], ew_win[:].bitcast(U32).indirect(lmk_sb[:, 16 * g : 16 * (g + 1)])
            )

        rs = []
        qsum = sbt("qsum", [P, NB], F32)
        lg = [sbt("lg%d" % tb, [P, V], F32) for tb in range(NB)]
        nc.gpsimd.memset(lg[0][:, 0:1], 0.0)
        a_all = []
        for h in range(2):
            a_sb = []
            a_all.append(a_sb)
            for g in range(2):
                y_ps = bank("y%d" % (2 * h + g), "y_ps%d%d" % (h, g), [P, 2, HALF])
                for i in range(2):
                    vb = 2 * g + i
                    nc.tensor.matmul_mx(
                        out=y_ps[:, i, :],
                        lhsT=eq[:, vb * P : (vb + 1) * P].bitcast(FP8X4), lhsT_scale=es[:, vb * P : (vb + 1) * P],
                        rhs=hq[h][:].bitcast(FP8X4), rhs_scale=hs[h][:],
                        start=True, stop=True,
                    )
                for i in range(2):
                    vb = 2 * g + i
                    at = sbt("a%d%d" % (h, vb), [P, HALF], F32)
                    if g == 0:
                        nc.scalar.activation(
                            at[:], y_ps[:, i, :], ACT.Identity, bias=y_bias[:, vb : vb + 1], scale=y_scale[:, vb : vb + 1]
                        )
                    else:
                        nc.vector.tensor_scalar(
                            at[:], y_ps[:, i, :], y_scale[:, vb : vb + 1], y_bias[:, vb : vb + 1], ALU.mult, ALU.add
                        )
                    a_sb.append(at)
        for h in range(2):
            a_sb = a_all[h]
            for i in range(2):
                tb = 2 * h + i
                for vb in range(NB):
                    nc.tensor.matmul(
                        u_ps[tb][:, vb * P : (vb + 1) * P], lhsT=a_sb[vb][:, i * P : (i + 1) * P], rhs=ident[:],
                        start=False, stop=(vb == NB - 1), is_transpose=True,
                    )
                rt = sbt("rs%d" % tb, [P, V], F32)
                nc.scalar.activation(rt[:], u_ps[tb][:], ACT.Abs_reciprocal_sqrt, bias=lg[0][:, 0:1])
                rs.append(rt)
                if tb == 1:
                    qn_first = sbt("qn_first", [P, V], F32)
                    nc.scalar.activation(qn_first[:], rs[0][:], ACT.Square, scale=V**-0.5, accum_out=qsum[:, 0:1])

        qn = sbt("qn", [P, V], F32, tag="y_bias")
        late = sbt("late", [P, 2, NB, V], F32, tag="y_scale")
        arg = late[:, 0]
        weight = late[:, 1]
        nc.vector.scalar_tensor_tensor(arg[:, 0, :], pij_sb[0], 0.05, u_ps[0][:], ALU.add, ALU.mult)
        for tb in range(1, NB):
            nc.vector.scalar_tensor_tensor(
                qn[:], rs[tb][:], inv_v[:], rs[tb][:], ALU.mult, ALU.mult, accum_out=qsum[:, tb : tb + 1]
            )
        qm = sbt("qm", [P, NB], F32)
        nc.vector.tensor_copy(qm[:], qsum[:])
        for tb in range(NB):
            nc.vector.tensor_tensor(weight[:, tb, :], pij_sb[tb], one_sb[:], ALU.mult)
            if tb + 1 < NB:
                nc.vector.scalar_tensor_tensor(
                    arg[:, tb + 1, :], pij_sb[tb + 1], 0.05, u_ps[tb + 1][:], ALU.add, ALU.mult
                )
        pieces = [(tb, 0, V) for tb in range(NB - 1)] + [(NB - 1, 0, HALF), (NB - 1, HALF, V)]
        for tb, c0, c1 in pieces:
            mean = qsum if tb == 0 else qm
            nc.scalar.activation(lg[tb][:, c0:c1], arg[:, tb, c0:c1], ACT.Ln, scale=mean[:, tb : tb + 1])
            res = sbt("res%d_%d" % (tb, c0), [P, c1 - c0], F32)
            nc.vector.scalar_tensor_tensor(
                res[:], lg[tb][:, c0:c1], prec_sb[:, tb : tb + 1], weight[:, tb, c0:c1], ALU.mult, ALU.mult
            )
            nc.sync.dma_start(out[tb * P : (tb + 1) * P, c0:c1], res[:])
